import numpy as np
import ml_dtypes


def mxq(x, axis, fmt="e4m3"):
    dtype, down = {"e4m3": (ml_dtypes.float8_e4m3fn, 7), "e5m2": (ml_dtypes.float8_e5m2, 14)}[fmt]
    v = np.moveaxis(np.asarray(x, np.float32).astype(ml_dtypes.bfloat16).astype(np.float64), axis, -1)
    blocks = v.reshape(v.shape[:-1] + (-1, 32))
    amax = np.abs(blocks).max(-1, keepdims=True)
    byte = np.maximum(np.where(amax > 0, np.frexp(amax)[1] - 1 + 127, 0) - down, 1)
    scale = np.exp2(byte - 127.0)
    codes = (blocks / scale).astype(np.float32).astype(dtype).astype(np.float64)
    return np.moveaxis((codes * scale).reshape(v.shape), -1, axis)


WIDE = False


def mx_kscale(k):
    if not WIDE:
        return np.ones(k)
    levels = np.array([10, -10, 5, -5, 0])
    if k % 512:
        return np.exp2(np.random.permutation(np.resize(levels, k // 32))).repeat(32)
    a = np.empty((k // 512, 16))
    for p in range(k // 512):
        a[p, :8] = np.random.permutation(np.resize(levels, 8))
        for g in range(8):
            far = levels[np.abs(levels - a[p, g]) >= 10]
            a[p, g + 8] = far[np.random.randint(len(far))]
    return np.exp2(a.ravel()).repeat(32)


def f64(x):
    return np.asarray(x).astype(np.float64)


def striped(idx):
    return np.tile(idx.reshape(-1, 16).T, (8, 1)).astype(np.uint16)


def unstriped(offs):
    return offs[:16].T.reshape(-1).astype(np.int64)


E2M1 = np.array([0.0, 0.5, 1.0, 1.5, 2.0, 3.0, 4.0, 6.0, -0.0, -0.5, -1.0, -1.5, -2.0, -3.0, -4.0, -6.0])


def pack_weight(w, fmt):
    k, n = w.shape
    w = f64(np.asarray(w, np.float32).astype(ml_dtypes.bfloat16)).reshape(k // 32, 32, n)
    amax = np.abs(w).max(1)
    if fmt == "e4m3":
        byte = np.frexp(amax)[1] - 1 + 127 - 7
    else:
        mant, ex = np.frexp(amax / 6.0)
        byte = np.where(mant > 0.5, ex, ex - 1) + 127
    byte = np.clip(np.where(amax > 0, byte, 1), 1, 254)
    scaled = (w * np.exp2(127.0 - byte)[:, None, :]).reshape(k, n).astype(np.float32)
    by_word = np.ascontiguousarray(scaled.reshape(k // 512, 128, 4, n).transpose(0, 1, 3, 2))
    if fmt == "e4m3":
        words = by_word.astype(ml_dtypes.float8_e4m3fn).view(np.uint8)
    else:
        c = by_word.astype(ml_dtypes.float4_e2m1fn).view(np.uint8) & 0xF
        words = (c[..., 0::2] | (c[..., 1::2] << 4)).reshape(k // 512, 128, 2 * n)
    return np.ascontiguousarray(words), np.ascontiguousarray(byte.astype(np.uint8).reshape(k // 512, 16, n))


def unpack_weight(words, scales, fmt):
    g, _, n = scales.shape
    words = np.ascontiguousarray(words).reshape(g, 128, n, -1)
    if fmt == "e4m3":
        vals = words.view(ml_dtypes.float8_e4m3fn).astype(np.float64)
    else:
        nib = np.empty((g, 128, n, 4), np.uint8)
        nib[..., 0::2] = words & 0xF
        nib[..., 1::2] = words >> 4
        vals = E2M1[nib]
    vals = vals * np.repeat(np.exp2(scales.astype(np.float64) - 127.0), 8, axis=1)[..., None]
    return vals.transpose(0, 1, 3, 2).reshape(g * 512, n)


def gelu(v):
    return 0.5 * v * (1.0 + np.tanh(np.sqrt(2.0 / np.pi) * (v + 0.044715 * v**3)))


K, H, N, T, S, T2, P = 1024, 1024, 768, 2048, 512, 1024, 512

def setup_inputs():
    n = np.random.standard_normal
    s = mx_kscale(K)[:, None]
    u = mx_kscale(H)[:, None]
    tab_words, tab_scales = pack_weight(n((K, T)) * s, "e4m3")
    w2_words, w2_scales = pack_weight(n((K, H)) / np.sqrt(K) / s, "e2m1")
    w4_words, w4_scales = pack_weight(n((H, N)) / np.sqrt(H) / u, "e4m3")
    return {
        "tab_words": tab_words, "tab_scales": tab_scales,
        "offs": striped(np.random.permutation(T)[:S]),
        "offs2": striped(np.random.permutation(T2)[:S]),
        "offs3": striped(np.random.permutation(T2)[:P]),
        "w1": (n((K, H)) / np.sqrt(K) / s * u.T).astype(np.float32),
        "w2_words": w2_words, "w2_scales": w2_scales,
        "wgs": np.exp(0.3 * n((128, S))).astype(np.float32),
        "page0": (n((H, T2)) * u).astype(np.float32),
        "sharp": (np.exp(0.3 * n(H)) / u[:, 0]).astype(np.float32),
        "gain": (np.exp(0.3 * n(H)) * u[:, 0]).astype(np.float32),
        "w3": (n((H, N)) / np.sqrt(H) / u).astype(np.float32),
        "w4_words": w4_words, "w4_scales": w4_scales,
    }

def reference(tab_words, tab_scales, offs, offs2, offs3, w1, w2_words, w2_scales, wgs, page0, sharp, gain, w3, w4_words, w4_scales):
    v = unpack_weight(tab_words, tab_scales, "e4m3")[:, unstriped(offs)]
    a = mxq(f64(w1), 0, "e4m3").T @ v
    b = unpack_weight(w2_words, w2_scales, "e2m1").T @ v
    h = a * b
    page = f64(page0).copy()
    page[:, unstriped(offs2)] = np.tile(f64(wgs), (H // 128, 1)) * h
    x = page[:, unstriped(offs3)]
    z = f64(gain)[:, None] * np.tanh(f64(sharp)[:, None] * x)
    zq = mxq(z, 0, "e4m3")
    xq = mxq(x, 0, "e4m3")
    return mxq(f64(w3), 0, "e4m3").T @ zq + unpack_weight(w4_words, w4_scales, "e4m3").T @ xq

@@ -1,0 +1,299 @@
+from contextlib import ExitStack
+
+import concourse.mybir as mybir
+
+K, H, N, T, S, T2, C = 1024, 1024, 768, 2048, 512, 1024, 512
+FLOPS = 2 * (2 * K * H * S + 2 * H * N * C)
+
+F32 = mybir.dt.float32
+BF16 = mybir.dt.bfloat16
+I32 = mybir.dt.int32
+U32 = mybir.dt.uint32
+U16 = mybir.dt.uint16
+U8 = mybir.dt.uint8
+FP8X4 = mybir.dt.float8_e4m3fn_x4
+FP4X4 = mybir.dt.float4_e2m1fn_x4
+MULT = mybir.AluOpType.mult
+TANH = mybir.ActivationFunctionType.Tanh
+COPY = mybir.ActivationFunctionType.Copy
+
+P = 128
+PACK = 4
+PASS = P * PACK
+KP = K // PASS
+HP = H // PASS
+NT = N // P
+QUADS = 4
+
+
+def tile_list_cart_board_completion_kernel(
+    tc, tab_words, tab_scales, offs, offs2, offs3, w1, w2_words, w2_scales, wgs, page0, sharp, gain, w3, w4_words, w4_scales, out
+):
+    nc = tc.nc
+    with ExitStack() as ctx:
+        keep = ctx.enter_context(tc.tile_pool(name="keep", bufs=1))
+        ring = ctx.enter_context(tc.tile_pool(name="ring", bufs=2))
+        psum = ctx.enter_context(tc.psum_pool(name="psum", bufs=1))
+
+        def cleared_plane(name, src):
+            plane = keep.tile([P, src.shape[0], src.shape[2]], U8, name=name, align_bytes=64)
+            nc.vector.memset(plane[:].rearrange("p a c -> p (a c)").bitcast(I32), 0)
+            return plane
+
+        def load_scales(plane, src):
+            for q in range(QUADS):
+                nc.sync.dma_start(
+                    out=plane[32 * q : 32 * q + 4, :, :].bitcast(I32),
+                    in_=src[:, 4 * q : 4 * q + 4, :].rearrange("a r c -> r a c").bitcast(I32),
+                )
+
+        def raw_rows(src, a, c0, width, slot):
+            raw = keep.tile([P, PACK, width], F32, name="raw", tag=slot)
+            nc.sync.dma_start(out=raw[:], in_=src[PASS * a : PASS * (a + 1), c0 : c0 + width].rearrange("(p j) c -> p j c", j=PACK))
+            return raw
+
+        def grouped_tile(width, slot):
+            return keep.tile([P, width * PACK], BF16, name="grouped", tag=slot, align_bytes=64)
+
+        def quantise(name, grouped, width, slot=None):
+            codes = keep.tile([P, width], U32, name=name + "_codes", tag=slot or name + "_codes", align_bytes=64)
+            scales = keep.tile([P, width], U8, name=name + "_scales", align_bytes=64)
+            for lo in range(0, width, PASS):
+                hi = min(lo + PASS, width)
+                nc.vector.quantize_mx(out=codes[:, lo:hi].bitcast(FP8X4), scales=scales[:, lo:hi], in_=grouped[:, PACK * lo : PACK * hi])
+            return codes, scales
+
+        def copy_on(engine, out, in_):
+            if engine == "scalar":
+                nc.scalar.copy(out=out, in_=in_)
+            else:
+                nc.vector.tensor_copy(out=out, in_=in_)
+
+        def weave(engine, rows, grouped):
+            copy_on(
+                engine,
+                grouped.rearrange("p (c i j) -> p c j i", i=4, j=PACK),
+                rows.rearrange("p j (c i) -> p c j i", i=4),
+            )
+
+        def woven(engine, rows, width, slot):
+            grouped = grouped_tile(width, slot)
+            weave(engine, rows, grouped[:])
+            return grouped
+
+        def weave_w1(raw, split, slot):
+            grouped = grouped_tile(PASS, slot)
+            dst = grouped[:].rearrange("p (t m j) -> p m j t", t=PACK, j=PACK)
+            src = raw[:].rearrange("p j (m t) -> p m j t", t=PACK)
+            if split > 0:
+                copy_on("vector", dst[:, :split], src[:, :split])
+            copy_on("scalar", dst[:, split:], src[:, split:])
+            return grouped
+
+        w2_plane_raw = cleared_plane("w2_plane_raw", w2_scales)
+        tab_plane = cleared_plane("tab_plane", tab_scales)
+        w4_plane = cleared_plane("w4_plane", w4_scales)
+        list1 = keep.tile([P, S // 16], U16, name="list1")
+        nc.sync.dma_start(list1[:], offs)
+        w2_raw = keep.tile([P, KP, 2 * H], U8, name="w2_raw", align_bytes=64)
+        nc.sync.dma_start(out=w2_raw[:].bitcast(I32), in_=w2_words.rearrange("a p c -> p a c").bitcast(I32))
+        load_scales(w2_plane_raw, w2_scales)
+        load_scales(tab_plane, tab_scales)
+        tab_sb = []
+        w1_raw = {}
+        for a in range(KP):
+            w1_raw[a, 0] = raw_rows(w1, a, 0, PASS, "raw%d" % a)
+            words = keep.tile([P, T], I32, name="tab%d" % a, align_bytes=64)
+            nc.sync.dma_start(out=words[:], in_=tab_words[a].rearrange("p t i -> p (t i)").bitcast(I32))
+            tab_sb.append(words)
+        list2 = keep.tile([P, S // 16], U16, name="list2")
+        nc.sync.dma_start(list2[:], offs2)
+        list3 = keep.tile([P, C // 16], U16, name="list3")
+        nc.sync.dma_start(list3[:], offs3)
+        wgs_rows = wgs.rearrange("(q t) s -> q t s", t=PACK)
+        wgs_first = keep.tile([P, 1, S], F32, name="wgs_first")
+        wgs_rest = keep.tile([P, PACK - 1, S], F32, name="wgs_rest")
+        for q in range(QUADS):
+            nc.sync.dma_start(out=wgs_first[32 * q : 32 * q + 32], in_=wgs_rows[:, 0:1, :])
+        pages = {}
+
+        def load_page(b, t):
+            pages[b, t] = keep.tile([P, T2], F32, name="page%d%d" % (b, t))
+            nc.sync.dma_start(out=pages[b, t][:], in_=page0[PASS * b : PASS * (b + 1), :].rearrange("(p t) c -> p t c", t=PACK)[:, t, :])
+
+        load_page(0, 0)
+        sharp_sb = keep.tile([P, HP, PACK], F32, name="sharp_sb")
+        gain_sb = keep.tile([P, HP, PACK], F32, name="gain_sb")
+        nc.sync.dma_start(out=sharp_sb[:], in_=sharp.rearrange("(b p t) -> p b t", b=HP, t=PACK))
+        nc.sync.dma_start(out=gain_sb[:], in_=gain.rearrange("(b p t) -> p b t", b=HP, t=PACK))
+        for q in range(QUADS):
+            nc.sync.dma_start(out=wgs_rest[32 * q : 32 * q + 32], in_=wgs_rows[:, 1:PACK, :])
+        w1_raw[0, 1] = raw_rows(w1, 0, PASS, PASS, "raw2")
+        load_page(0, 1)
+        w1_raw[1, 1] = raw_rows(w1, 1, PASS, PASS, "raw3")
+        load_page(0, 2)
+        w3_raw = {}
+        w3_grouped = {}
+
+        def load_w3(b):
+            w3_raw[b, 0] = raw_rows(w3, b, 0, PASS, "raw%d" % (4 + b))
+            w3_raw[b, PASS] = raw_rows(w3, b, PASS, N - PASS, "raw_narrow%d" % b)
+
+        w2_sb = keep.tile([P, KP * HP, 2 * PASS], U8, name="w2_sb", align_bytes=64)
+        w2_plane = keep.tile([P, KP * HP, PASS], U8, name="w2_plane", align_bytes=64)
+        nc.vector.tensor_copy(
+            out=w2_sb[:].bitcast(U16).rearrange("p g (t m) -> p g m t", t=PACK),
+            in_=w2_raw[:].bitcast(U16).rearrange("p a (b m t) -> p (a b) m t", b=HP, t=PACK),
+        )
+        nc.vector.tensor_copy(
+            out=w2_plane[:].rearrange("p g (t m) -> p g m t", t=PACK),
+            in_=w2_plane_raw[:].rearrange("p a (b m t) -> p (a b) m t", b=HP, t=PACK),
+        )
+
+        v_codes, v_scales = [], []
+        for a in range(KP):
+            scales = keep.tile([P, S], U8, name="v_scales%d" % a, align_bytes=64)
+            nc.vector.tensor_copy(scales[:], tab_plane[:, a, :].indirect(list1[:]))
+            v_scales.append(scales)
+
+        def gather_words(a):
+            codes = keep.tile([P, S], I32, name="v_codes%d" % a, align_bytes=64)
+            nc.vector.tensor_copy(codes[:].bitcast(U32), tab_sb[a][:].bitcast(U32).indirect(list1[:]))
+            v_codes.append(codes)
+
+        w1_q = {}
+        w1_grouped = {}
+        w3_q = {}
+
+        def weave_w3(b, c0):
+            if c0 == 0:
+                w3_grouped[b] = grouped_tile(N, "grouped_w3%d" % b)
+            raw = w3_raw[b, c0]
+            weave("scalar", raw[:], w3_grouped[b][:, PACK * c0 : PACK * (c0 + raw.shape[2])])
+
+        def first_stage(b, t, slot):
+            cols = slice(P * t, P * (t + 1))
+            acc_a = psum.tile([P, S], F32, name="acc_a", tag="acc_a")
+            acc_b = psum.tile([P, S], F32, name="acc_b", tag="acc_b")
+            for a in range(KP):
+                codes, scales = w1_q[a, b]
+                for acc, lhs, lhs_scale in (
+                    (acc_a, codes[:, cols].bitcast(FP8X4), scales[:, cols]),
+                    (acc_b, w2_sb[:, a * HP + b, 2 * P * t : 2 * P * (t + 1)].bitcast(FP4X4), w2_plane[:, a * HP + b, cols]),
+                ):
+                    nc.tensor.matmul_mx(
+                        out=acc[:],
+                        lhsT=lhs,
+                        lhsT_scale=lhs_scale,
+                        rhs=v_codes[a][:].bitcast(FP8X4),
+                        rhs_scale=v_scales[a][:],
+                        start=(a == 0),
+                        stop=(a == KP - 1),
+                    )
+            affinity = ring.tile([P, S], F32, name="affinity")
+            nc.scalar.copy(out=affinity[:], in_=acc_b[:])
+            weighted = keep.tile([P, S], F32, name="weighted", tag=slot, align_bytes=64)
+            wgs_t = wgs_first[:, 0, :] if t == 0 else wgs_rest[:, t - 1, :]
+            nc.vector.tensor_tensor(weighted[:], acc_a[:], wgs_t, MULT)
+            return weighted, affinity
+
+        accs = [psum.tile([P, C], F32, name="out%d" % n, tag="out%d" % n) for n in range(NT)]
+
+        def second_stage(b, which, moving, c_lo=0, c_hi=C):
+            codes, scales = moving
+            for n in range(NT):
+                if which == "x":
+                    lhs, lhs_scale = w4_sb[:, b, P * n : P * (n + 1)], w4_plane[:, b, P * n : P * (n + 1)]
+                else:
+                    wc, ws = w3_q[b]
+                    lhs, lhs_scale = wc[:, P * n : P * (n + 1)], ws[:, P * n : P * (n + 1)]
+                nc.tensor.matmul_mx(
+                    out=accs[n][:, c_lo:c_hi],
+                    lhsT=lhs.bitcast(FP8X4),
+                    lhsT_scale=lhs_scale,
+                    rhs=codes[:].bitcast(FP8X4),
+                    rhs_scale=scales[:],
+                    start=(b == 0 and which == "z"),
+                    stop=(b == HP - 1 and which == "z" and c_hi == C),
+                )
+
+        gather_words(0)
+        w1_q[0, 0] = quantise("w1q00", weave_w1(w1_raw[0, 0], 0, "grouped0"), PASS)
+        w1_q[1, 0] = quantise("w1q10", weave_w1(w1_raw[1, 0], 80, "grouped1"), PASS)
+        gather_words(1)
+        load_w3(0)
+        load_page(0, 3)
+        load_w3(1)
+        load_page(1, 0)
+        load_scales(w4_plane, w4_scales)
+        w4_sb = keep.tile([P, HP, N], I32, name="w4_sb", align_bytes=64)
+        nc.sync.dma_start(out=w4_sb[:], in_=w4_words.rearrange("a p c i -> p a (c i)").bitcast(I32))
+        for t in range(1, PACK):
+            load_page(1, t)
+
+        slices = [(b, t) for b in range(HP) for t in range(PACK)]
+        xs = [keep.tile([P, PACK, C], F32, name="xs%d" % b) for b in range(HP)]
+        zs = [keep.tile([P, PACK, C], BF16, name="zs%d" % b) for b in range(HP)]
+        bent_slot = {1: "raw3", 2: "raw4", 3: "raw5"}
+        weighted_slot = {6: "grouped0"}
+
+        def read_page(i, lo, hi):
+            b, t = slices[i]
+            nc.vector.tensor_copy(xs[b][:, t, lo:hi], pages[b, t][:].indirect(list3[:, lo // 16 : hi // 16]))
+            bent = keep.tile([P, hi - lo], F32, name="bent", tag=bent_slot.get(i, "bent%d" % (lo // half)))
+            nc.scalar.activation(out=bent[:], in_=xs[b][:, t, lo:hi], func=TANH, scale=sharp_sb[:, b, t : t + 1])
+            nc.scalar.activation(out=zs[b][:, t, lo:hi], in_=bent[:], func=COPY, scale=gain_sb[:, b, t : t + 1])
+
+        half = C // 2
+        grouped = {}
+        ready = first_stage(0, 0, "weighted0")
+        for i, (b, t) in enumerate(slices):
+            weighted, affinity = ready
+            nc.vector.tensor_tensor(pages[b, t][:].indirect(list2[:]), weighted[:], affinity[:], MULT)
+            if i + 1 == len(slices):
+                break
+            ready = first_stage(*slices[i + 1], weighted_slot.get(i + 1, "weighted%d" % (i + 1)))
+            if i == 0:
+                w1_grouped[0] = weave_w1(w1_raw[0, 1], 0, "grouped0")
+            if i == 1:
+                w1_grouped[1] = weave_w1(w1_raw[1, 1], 0, "grouped1")
+            if i == 2:
+                weave_w3(0, 0)
+            if i == 3:
+                weave_w3(0, PASS)
+                weave_w3(1, 0)
+            read_page(i, 0, C)
+            if i == 1:
+                w1_q[0, 1] = quantise("w1q01", w1_grouped[0], PASS, "weighted1")
+            if i == 2:
+                w1_q[1, 1] = quantise("w1q11", w1_grouped[1], PASS, "weighted2")
+            if i == 3:
+                grouped["x"] = woven("scalar", xs[0][:], C, "grouped0")
+                w3_q[0] = quantise("w3q0", w3_grouped[0], N, "weighted3")
+            if i == 4:
+                grouped["z"] = woven("scalar", zs[0][:], C, "grouped1")
+                weave_w3(1, PASS)
+                qx0 = quantise("xq0", grouped["x"], C, "weighted4")
+            if i == 5:
+                w3_q[1] = quantise("w3q1", w3_grouped[1], N, "weighted5")
+            if i == 6:
+                second_stage(0, "z", quantise("zq0", grouped["z"], C, "grouped0"))
+                second_stage(0, "x", qx0)
+        last = len(slices) - 1
+        read_page(last, 0, half)
+        gx0 = woven("vector", xs[1][:, :, 0:half], half, "tail0")
+        gz0 = woven("scalar", zs[1][:, :, 0:half], half, "tail1")
+        read_page(last, half, C)
+        second_stage(1, "x", quantise("xq1a", gx0, half), 0, half)
+        gx1 = woven("vector", xs[1][:, :, half:C], half, "tail2")
+        qz0 = quantise("zq1a", gz0, half)
+        qx1 = quantise("xq1b", gx1, half)
+        gz1 = woven("vector", zs[1][:, :, half:C], half, "tail3")
+        second_stage(1, "z", qz0, 0, half)
+        second_stage(1, "x", qx1, half, C)
+        qz1 = quantise("zq1b", gz1, half)
+        second_stage(1, "z", qz1, half, C)
+        for n in range(NT):
+            result = keep.tile([P, C], F32, name="result", tag="raw%d" % n)
+            copy_on("scalar" if n % 2 == 0 else "vector", result[:], accs[n][:])
+            nc.sync.dma_start(out=out[P * n : P * (n + 1), :], in_=result[:])

@@ -14,6 +14,7 @@ U8 = mybir.dt.uint8
 FP8X4 = mybir.dt.float8_e4m3fn_x4
 FP4X4 = mybir.dt.float4_e2m1fn_x4
 MULT = mybir.AluOpType.mult
+ADD = mybir.AluOpType.add
 TANH = mybir.ActivationFunctionType.Tanh
 COPY = mybir.ActivationFunctionType.Copy
 
@@ -35,29 +36,29 @@ def tile_list_cart_board_completion_kernel(
         ring = ctx.enter_context(tc.tile_pool(name="ring", bufs=2))
         psum = ctx.enter_context(tc.psum_pool(name="psum", bufs=1))
 
-        def cleared_plane(name, src):
-            plane = keep.tile([P, src.shape[0], src.shape[2]], U8, name=name, align_bytes=64)
-            nc.vector.memset(plane[:].rearrange("p a c -> p (a c)").bitcast(I32), 0)
+        def tile(shape, dtype, name, slot=None):
+            return keep.tile(shape, dtype, name=name, tag=slot or name, align_bytes=64)
+
+        def cleared(name, width):
+            plane = tile([P, width], U8, name)
+            nc.vector.memset(plane[:].bitcast(I32), 0)
             return plane
 
         def load_scales(plane, src):
             for q in range(QUADS):
-                nc.sync.dma_start(
-                    out=plane[32 * q : 32 * q + 4, :, :].bitcast(I32),
-                    in_=src[:, 4 * q : 4 * q + 4, :].rearrange("a r c -> r a c").bitcast(I32),
-                )
+                nc.scalar.dma_start(out=plane[32 * q : 32 * q + 8, :].bitcast(I32), in_=src[:, 4 * q : 4 * q + 4, :].bitcast(I32))
+
+        def second_plane(packed, shifted):
+            nc.gpsimd.dma_start(out=shifted[0 : P - 4, :].bitcast(I32), in_=packed[4:P, :].bitcast(I32))
 
         def raw_rows(src, a, c0, width, slot):
-            raw = keep.tile([P, PACK, width], F32, name="raw", tag=slot)
+            raw = tile([P, PACK, width], F32, "raw", slot)
             nc.sync.dma_start(out=raw[:], in_=src[PASS * a : PASS * (a + 1), c0 : c0 + width].rearrange("(p j) c -> p j c", j=PACK))
             return raw
 
-        def grouped_tile(width, slot):
-            return keep.tile([P, width * PACK], BF16, name="grouped", tag=slot, align_bytes=64)
-
         def quantise(name, grouped, width, slot=None):
-            codes = keep.tile([P, width], U32, name=name + "_codes", tag=slot or name + "_codes", align_bytes=64)
-            scales = keep.tile([P, width], U8, name=name + "_scales", align_bytes=64)
+            codes = tile([P, width], U32, name + "_codes", slot)
+            scales = tile([P, width], U8, name + "_scales")
             for lo in range(0, width, PASS):
                 hi = min(lo + PASS, width)
                 nc.vector.quantize_mx(out=codes[:, lo:hi].bitcast(FP8X4), scales=scales[:, lo:hi], in_=grouped[:, PACK * lo : PACK * hi])
@@ -77,33 +78,37 @@ def tile_list_cart_board_completion_kernel(
             )
 
         def woven(engine, rows, width, slot):
-            grouped = grouped_tile(width, slot)
+            grouped = tile([P, width * PACK], BF16, "grouped", slot)
             weave(engine, rows, grouped[:])
             return grouped
 
-        def weave_w1(raw, split, slot):
-            grouped = grouped_tile(PASS, slot)
-            dst = grouped[:].rearrange("p (t m j) -> p m j t", t=PACK, j=PACK)
-            src = raw[:].rearrange("p j (m t) -> p m j t", t=PACK)
-            if split > 0:
-                copy_on("vector", dst[:, :split], src[:, :split])
-            copy_on("scalar", dst[:, split:], src[:, split:])
+        def woven_w1(engine, raw, slot):
+            grouped = tile([P, PASS * PACK], BF16, "grouped", slot)
+            copy_on(
+                engine,
+                grouped[:].rearrange("p (t m j) -> p m j t", t=PACK, j=PACK),
+                raw[:].rearrange("p j (m t) -> p m j t", t=PACK),
+            )
             return grouped
 
-        w2_plane_raw = cleared_plane("w2_plane_raw", w2_scales)
-        tab_plane = cleared_plane("tab_plane", tab_scales)
-        w4_plane = cleared_plane("w4_plane", w4_scales)
+        w2_plane_raw = cleared("w2_plane_raw", H)
+        tab_plane = cleared("tab_plane", T)
+        w2_shifted = cleared("w2_shifted", H)
+        v_shifted = cleared("v_shifted", S)
+        w4_plane = cleared("w4_plane", N)
         list1 = keep.tile([P, S // 16], U16, name="list1")
         nc.sync.dma_start(list1[:], offs)
-        w2_raw = keep.tile([P, KP, 2 * H], U8, name="w2_raw", align_bytes=64)
+        w2_raw = tile([P, KP, 2 * H], U8, "w2_raw")
         nc.sync.dma_start(out=w2_raw[:].bitcast(I32), in_=w2_words.rearrange("a p c -> p a c").bitcast(I32))
         load_scales(w2_plane_raw, w2_scales)
         load_scales(tab_plane, tab_scales)
-        tab_sb = []
+        load_scales(w4_plane, w4_scales)
         w1_raw = {}
         for a in range(KP):
             w1_raw[a, 0] = raw_rows(w1, a, 0, PASS, "raw%d" % a)
-            words = keep.tile([P, T], I32, name="tab%d" % a, align_bytes=64)
+        tab_sb = []
+        for a in range(KP):
+            words = tile([P, T], I32, "tab%d" % a)
             nc.sync.dma_start(out=words[:], in_=tab_words[a].rearrange("p t i -> p (t i)").bitcast(I32))
             tab_sb.append(words)
         list2 = keep.tile([P, S // 16], U16, name="list2")
@@ -111,189 +116,237 @@ def tile_list_cart_board_completion_kernel(
         list3 = keep.tile([P, C // 16], U16, name="list3")
         nc.sync.dma_start(list3[:], offs3)
         wgs_rows = wgs.rearrange("(q t) s -> q t s", t=PACK)
-        wgs_first = keep.tile([P, 1, S], F32, name="wgs_first")
-        wgs_rest = keep.tile([P, PACK - 1, S], F32, name="wgs_rest")
+        wgs_first = tile([P, 1, S], F32, "wgs_first")
         for q in range(QUADS):
             nc.sync.dma_start(out=wgs_first[32 * q : 32 * q + 32], in_=wgs_rows[:, 0:1, :])
         pages = {}
 
         def load_page(b, t):
-            pages[b, t] = keep.tile([P, T2], F32, name="page%d%d" % (b, t))
+            pages[b, t] = tile([P, T2], F32, "page%d%d" % (b, t))
             nc.sync.dma_start(out=pages[b, t][:], in_=page0[PASS * b : PASS * (b + 1), :].rearrange("(p t) c -> p t c", t=PACK)[:, t, :])
 
+        w3_raw = {}
+
+        def load_w3(b, c0):
+            w3_raw[b, c0] = raw_rows(w3, b, c0, min(PASS, N - c0), ("raw_narrow%d" % b) if c0 else "raw%d" % (4 + b))
+
         load_page(0, 0)
-        sharp_sb = keep.tile([P, HP, PACK], F32, name="sharp_sb")
-        gain_sb = keep.tile([P, HP, PACK], F32, name="gain_sb")
+        load_page(0, 1)
+        sharp_sb = tile([P, HP, PACK], F32, "sharp_sb")
+        gain_sb = tile([P, HP, PACK], F32, "gain_sb")
         nc.sync.dma_start(out=sharp_sb[:], in_=sharp.rearrange("(b p t) -> p b t", b=HP, t=PACK))
         nc.sync.dma_start(out=gain_sb[:], in_=gain.rearrange("(b p t) -> p b t", b=HP, t=PACK))
-        for q in range(QUADS):
-            nc.sync.dma_start(out=wgs_rest[32 * q : 32 * q + 32], in_=wgs_rows[:, 1:PACK, :])
         w1_raw[0, 1] = raw_rows(w1, 0, PASS, PASS, "raw2")
-        load_page(0, 1)
         w1_raw[1, 1] = raw_rows(w1, 1, PASS, PASS, "raw3")
+        load_w3(0, 0)
         load_page(0, 2)
-        w3_raw = {}
-        w3_grouped = {}
+        load_w3(0, PASS)
+        load_page(0, 3)
+        load_w3(1, 0)
+        load_page(1, 0)
+        load_w3(1, PASS)
+        load_page(1, 1)
+        w4_sb = tile([P, HP, N], I32, "w4_sb")
+        nc.sync.dma_start(out=w4_sb[:], in_=w4_words.rearrange("a p c i -> p a (c i)").bitcast(I32))
+        load_page(1, 2)
+        load_page(1, 3)
 
-        def load_w3(b):
-            w3_raw[b, 0] = raw_rows(w3, b, 0, PASS, "raw%d" % (4 + b))
-            w3_raw[b, PASS] = raw_rows(w3, b, PASS, N - PASS, "raw_narrow%d" % b)
-
-        w2_sb = keep.tile([P, KP * HP, 2 * PASS], U8, name="w2_sb", align_bytes=64)
-        w2_plane = keep.tile([P, KP * HP, PASS], U8, name="w2_plane", align_bytes=64)
+        w2_sb = tile([P, KP * HP, 2 * PASS], U8, "w2_sb")
+        w2_plane = tile([P, H], U8, "w2_plane")
+        nc.vector.tensor_copy(
+            out=w2_plane[:].rearrange("p (b t m) -> p b m t", b=HP, t=PACK),
+            in_=w2_plane_raw[:].rearrange("p (b m t) -> p b m t", b=HP, t=PACK),
+        )
+        second_plane(w2_plane, w2_shifted)
+        v_plane = tile([P, S], U8, "v_plane")
+        nc.vector.tensor_copy(v_plane[:], tab_plane[:].indirect(list1[:]))
+        second_plane(v_plane, v_shifted)
         nc.vector.tensor_copy(
             out=w2_sb[:].bitcast(U16).rearrange("p g (t m) -> p g m t", t=PACK),
             in_=w2_raw[:].bitcast(U16).rearrange("p a (b m t) -> p (a b) m t", b=HP, t=PACK),
         )
-        nc.vector.tensor_copy(
-            out=w2_plane[:].rearrange("p g (t m) -> p g m t", t=PACK),
-            in_=w2_plane_raw[:].rearrange("p a (b m t) -> p (a b) m t", b=HP, t=PACK),
-        )
-
-        v_codes, v_scales = [], []
-        for a in range(KP):
-            scales = keep.tile([P, S], U8, name="v_scales%d" % a, align_bytes=64)
-            nc.vector.tensor_copy(scales[:], tab_plane[:, a, :].indirect(list1[:]))
-            v_scales.append(scales)
+        v_codes = []
 
         def gather_words(a):
-            codes = keep.tile([P, S], I32, name="v_codes%d" % a, align_bytes=64)
+            codes = tile([P, S], I32, "v_codes%d" % a)
             nc.vector.tensor_copy(codes[:].bitcast(U32), tab_sb[a][:].bitcast(U32).indirect(list1[:]))
             v_codes.append(codes)
 
         w1_q = {}
-        w1_grouped = {}
         w3_q = {}
+        w3_grouped = [tile([P, N * PACK], BF16, "grouped_w3%d" % b) for b in range(HP)]
 
         def weave_w3(b, c0):
-            if c0 == 0:
-                w3_grouped[b] = grouped_tile(N, "grouped_w3%d" % b)
             raw = w3_raw[b, c0]
             weave("scalar", raw[:], w3_grouped[b][:, PACK * c0 : PACK * (c0 + raw.shape[2])])
 
-        def first_stage(b, t, slot):
+        slices = [(b, t) for b in range(HP) for t in range(PACK)]
+        contents_slot = {}
+        bent_slot = {i: contents_slot.get(i + 2, "contents%d" % (i + 2)) for i in range(6)}
+
+        def first_stage(i):
+            b, t = slices[i]
             cols = slice(P * t, P * (t + 1))
+            wide = slice(PASS * b + P * t, PASS * b + P * (t + 1))
             acc_a = psum.tile([P, S], F32, name="acc_a", tag="acc_a")
             acc_b = psum.tile([P, S], F32, name="acc_b", tag="acc_b")
-            for a in range(KP):
-                codes, scales = w1_q[a, b]
-                for acc, lhs, lhs_scale in (
-                    (acc_a, codes[:, cols].bitcast(FP8X4), scales[:, cols]),
-                    (acc_b, w2_sb[:, a * HP + b, 2 * P * t : 2 * P * (t + 1)].bitcast(FP4X4), w2_plane[:, a * HP + b, cols]),
-                ):
-                    nc.tensor.matmul_mx(
-                        out=acc[:],
-                        lhsT=lhs,
-                        lhsT_scale=lhs_scale,
-                        rhs=v_codes[a][:].bitcast(FP8X4),
-                        rhs_scale=v_scales[a][:],
-                        start=(a == 0),
-                        stop=(a == KP - 1),
-                    )
-            affinity = ring.tile([P, S], F32, name="affinity")
-            nc.scalar.copy(out=affinity[:], in_=acc_b[:])
-            weighted = keep.tile([P, S], F32, name="weighted", tag=slot, align_bytes=64)
+            passes = [(name, a) for a in range(KP) for name in "ab"] if i == 0 else [(name, a) for name in "ba" for a in range(KP)]
+            for name, a in passes:
+                if name == "a":
+                    acc, lhs, lhs_scale = acc_a, w1_q[a, b][0][:, cols].bitcast(FP8X4), w1_q[a, b][1][:, cols]
+                    rhs_scale = v_plane[4 * a : P, :]
+                else:
+                    acc, lhs = acc_b, w2_sb[:, a * HP + b, 2 * P * t : 2 * P * (t + 1)].bitcast(FP4X4)
+                    lhs_scale, rhs_scale = (w2_plane, w2_shifted)[a][:, wide], (v_plane, v_shifted)[a][:]
+                nc.tensor.matmul_mx(
+                    out=acc[:],
+                    lhsT=lhs,
+                    lhsT_scale=lhs_scale,
+                    rhs=v_codes[a][:].bitcast(FP8X4),
+                    rhs_scale=rhs_scale,
+                    start=(a == 0),
+                    stop=(a == KP - 1),
+                )
             wgs_t = wgs_first[:, 0, :] if t == 0 else wgs_rest[:, t - 1, :]
-            nc.vector.tensor_tensor(weighted[:], acc_a[:], wgs_t, MULT)
+            weighted = ring.tile([P, S], F32, name="weighted", bufs=3)
+            if i == 0:
+                put = tile([P, S], F32, "put0")
+                nc.vector.tensor_tensor(weighted[:], acc_a[:], wgs_t, MULT)
+                nc.vector.tensor_tensor(put[:], acc_b[:], weighted[:], MULT)
+                return put
+            contents = tile([P, S], F32, "contents", contents_slot.get(i, "contents%d" % i))
+            nc.scalar.copy(out=contents[:], in_=acc_a[:])
+            affinity = tile([P, S], F32, "affinity%d" % i)
+            nc.scalar.copy(out=affinity[:], in_=acc_b[:])
+            nc.gpsimd.tensor_tensor(weighted[:], contents[:], wgs_t, MULT)
             return weighted, affinity
+
+        def product(i, weighted, contents):
+            put = tile([P, S], F32, "put", "zs0" if i == last else "put%d" % (i % 2))
+            nc.gpsimd.tensor_tensor(put[:], weighted[:], contents[:], MULT)
+            return put
 
         accs = [psum.tile([P, C], F32, name="out%d" % n, tag="out%d" % n) for n in range(NT)]
 
         def second_stage(b, which, moving, c_lo=0, c_hi=C):
             codes, scales = moving
             for n in range(NT):
+                cols = slice(P * n, P * (n + 1))
                 if which == "x":
-                    lhs, lhs_scale = w4_sb[:, b, P * n : P * (n + 1)], w4_plane[:, b, P * n : P * (n + 1)]
+                    lhs, lhs_scale = w4_sb[:, b, cols], w4_plane[4 * b : P, cols]
                 else:
-                    wc, ws = w3_q[b]
-                    lhs, lhs_scale = wc[:, P * n : P * (n + 1)], ws[:, P * n : P * (n + 1)]
+                    c0 = P * n // PASS * PASS
+                    lhs, lhs_scale = (part[:, P * n - c0 : P * (n + 1) - c0] for part in w3_q[b, c0])
                 nc.tensor.matmul_mx(
                     out=accs[n][:, c_lo:c_hi],
                     lhsT=lhs.bitcast(FP8X4),
                     lhsT_scale=lhs_scale,
-                    rhs=codes[:].bitcast(FP8X4),
-                    rhs_scale=scales[:],
+                    rhs=codes[:, c_lo:c_hi].bitcast(FP8X4),
+                    rhs_scale=scales[:, c_lo:c_hi],
                     start=(b == 0 and which == "z"),
                     stop=(b == HP - 1 and which == "z" and c_hi == C),
                 )
 
+        w1_q[0, 0] = quantise("w1q00", woven_w1("vector", w1_raw[0, 0], "grouped0"), PASS)
+        grouped = woven_w1("scalar", w1_raw[1, 0], "grouped1")
         gather_words(0)
-        w1_q[0, 0] = quantise("w1q00", weave_w1(w1_raw[0, 0], 0, "grouped0"), PASS)
-        w1_q[1, 0] = quantise("w1q10", weave_w1(w1_raw[1, 0], 80, "grouped1"), PASS)
+        wgs_rest = tile([P, PACK - 1, S], F32, "wgs_rest", "tab0")
+        for q in range(QUADS):
+            nc.scalar.dma_start(out=wgs_rest[32 * q : 32 * q + 32], in_=wgs_rows[:, 1:PACK, :])
+        w1_q[1, 0] = quantise("w1q10", grouped, PASS)
         gather_words(1)
-        load_w3(0)
-        load_page(0, 3)
-        load_w3(1)
-        load_page(1, 0)
-        load_scales(w4_plane, w4_scales)
-        w4_sb = keep.tile([P, HP, N], I32, name="w4_sb", align_bytes=64)
-        nc.sync.dma_start(out=w4_sb[:], in_=w4_words.rearrange("a p c i -> p a (c i)").bitcast(I32))
-        for t in range(1, PACK):
-            load_page(1, t)
 
-        slices = [(b, t) for b in range(HP) for t in range(PACK)]
-        xs = [keep.tile([P, PACK, C], F32, name="xs%d" % b) for b in range(HP)]
-        zs = [keep.tile([P, PACK, C], BF16, name="zs%d" % b) for b in range(HP)]
-        bent_slot = {1: "raw3", 2: "raw4", 3: "raw5"}
-        weighted_slot = {6: "grouped0"}
+        xs = [tile([P, PACK, C], F32, "xs0"), tile([P, PACK, C], F32, "xs1", "raw0")]
+        zs = [tile([P, PACK, C], BF16, "zs0"), tile([P, PACK, C], BF16, "zs1", "w2_raw")]
+        half = C // 2
+        last = len(slices) - 1
 
         def read_page(i, lo, hi):
             b, t = slices[i]
             nc.vector.tensor_copy(xs[b][:, t, lo:hi], pages[b, t][:].indirect(list3[:, lo // 16 : hi // 16]))
-            bent = keep.tile([P, hi - lo], F32, name="bent", tag=bent_slot.get(i, "bent%d" % (lo // half)))
+            bent = tile([P, hi - lo], F32, "bent", bent_slot.get(i, "bent%d" % (i % 2 + lo // half)))
             nc.scalar.activation(out=bent[:], in_=xs[b][:, t, lo:hi], func=TANH, scale=sharp_sb[:, b, t : t + 1])
-            nc.scalar.activation(out=zs[b][:, t, lo:hi], in_=bent[:], func=COPY, scale=gain_sb[:, b, t : t + 1])
+            if i == last:
+                nc.scalar.activation(out=zs[b][:, t, lo:hi], in_=bent[:], func=COPY, scale=gain_sb[:, b, t : t + 1])
+            else:
+                nc.gpsimd.tensor_scalar(zs[b][:, t, lo:hi], bent[:], gain_sb[:, b, t : t + 1], 0.0, MULT, ADD)
 
-        half = C // 2
+        def codes_slot(i):
+            return "affinity%d" % i
+
+        def weave_pair(engine, rows, grouped, j, lo, hi):
+            copy_on(
+                engine,
+                grouped[:, PACK * lo : PACK * hi].rearrange("p (c i j) -> p c j i", i=4, j=PACK)[:, :, j : j + 2, :],
+                rows[:, j : j + 2, lo:hi].rearrange("p j (c i) -> p c j i", i=4),
+            )
+
+        def quantise_into(target, grouped, lo, hi):
+            codes, scales = target
+            nc.vector.quantize_mx(out=codes[:, lo:hi].bitcast(FP8X4), scales=scales[:, lo:hi], in_=grouped[:, PACK * lo : PACK * hi])
+
+        puts = {0: first_stage(0), 1: product(1, *first_stage(1))}
+        parts = {}
+        weave_at = {0: (0, 1), 2: (2,), 3: (3,)}
+        w3_pieces = [(0, 0), (0, PASS), (1, 0), (1, PASS)]
+        products_after = {0: (2,), 1: (3, 4), 2: (5,), 3: (6, 7)}
         grouped = {}
-        ready = first_stage(0, 0, "weighted0")
+        gx = tile([P, C * PACK], BF16, "gx", "raw1")
+        gz = tile([P, C * PACK], BF16, "gz", "tab1")
         for i, (b, t) in enumerate(slices):
-            weighted, affinity = ready
-            nc.vector.tensor_tensor(pages[b, t][:].indirect(list2[:]), weighted[:], affinity[:], MULT)
-            if i + 1 == len(slices):
+            nc.vector.tensor_copy(pages[b, t][:].indirect(list2[:]), puts[i][:])
+            if i == last:
                 break
-            ready = first_stage(*slices[i + 1], weighted_slot.get(i + 1, "weighted%d" % (i + 1)))
             if i == 0:
-                w1_grouped[0] = weave_w1(w1_raw[0, 1], 0, "grouped0")
+                grouped["w1a"] = woven_w1("scalar", w1_raw[0, 1], "grouped0")
+                grouped["w1b"] = woven_w1("scalar", w1_raw[1, 1], "grouped1")
             if i == 1:
-                w1_grouped[1] = weave_w1(w1_raw[1, 1], 0, "grouped1")
-            if i == 2:
-                weave_w3(0, 0)
-            if i == 3:
-                weave_w3(0, PASS)
-                weave_w3(1, 0)
+                codes = tile([P, KP * PASS], U32, "w1q_codes", codes_slot(i))
+                scales = tile([P, KP * PASS], U8, "w1q_scales")
+                for a, name in enumerate(("w1a", "w1b")):
+                    w1_q[a, 1] = codes[:, PASS * a : PASS * (a + 1)], scales[:, PASS * a : PASS * (a + 1)]
+                    quantise_into(w1_q[a, 1], grouped[name], 0, PASS)
+            for piece in weave_at.get(i, ()):
+                weave_w3(*w3_pieces[piece])
+            if 2 <= i <= 5:
+                wb, c0 = w3_pieces[i - 2]
+                width = w3_raw[wb, c0].shape[2]
+                w3_q[wb, c0] = quantise("w3q%d" % i, w3_grouped[wb][:, PACK * c0 : PACK * (c0 + width)], width, codes_slot(i))
+            if i == 6:
+                qx0 = quantise("xq0", grouped["x"], C, codes_slot(i))
+            for ahead in products_after.get(i, ()):
+                parts[ahead] = first_stage(ahead)
+            if i + 2 <= last:
+                puts[i + 2] = product(i + 2, *parts[i + 2])
             read_page(i, 0, C)
-            if i == 1:
-                w1_q[0, 1] = quantise("w1q01", w1_grouped[0], PASS, "weighted1")
-            if i == 2:
-                w1_q[1, 1] = quantise("w1q11", w1_grouped[1], PASS, "weighted2")
             if i == 3:
                 grouped["x"] = woven("scalar", xs[0][:], C, "grouped0")
-                w3_q[0] = quantise("w3q0", w3_grouped[0], N, "weighted3")
-            if i == 4:
                 grouped["z"] = woven("scalar", zs[0][:], C, "grouped1")
-                weave_w3(1, PASS)
-                qx0 = quantise("xq0", grouped["x"], C, "weighted4")
             if i == 5:
-                w3_q[1] = quantise("w3q1", w3_grouped[1], N, "weighted5")
+                weave_pair("scalar", xs[1], gx, 0, 0, C)
+                weave_pair("scalar", zs[1], gz, 0, 0, C)
             if i == 6:
-                second_stage(0, "z", quantise("zq0", grouped["z"], C, "grouped0"))
+                z_codes = tile([P, C], U32, "z_codes", "put0")
+                z_scales = tile([P, C], U8, "zq0_scales")
+                quantise_into((z_codes, z_scales), grouped["z"], 0, C)
+                second_stage(0, "z", (z_codes, z_scales))
                 second_stage(0, "x", qx0)
-        last = len(slices) - 1
+        qx1 = tile([P, C], U32, "xq1_codes"), tile([P, C], U8, "xq1_scales")
+        qz1 = tile([P, C], U32, "zq1_codes"), tile([P, C], U8, "zq1_scales")
         read_page(last, 0, half)
-        gx0 = woven("vector", xs[1][:, :, 0:half], half, "tail0")
-        gz0 = woven("scalar", zs[1][:, :, 0:half], half, "tail1")
         read_page(last, half, C)
-        second_stage(1, "x", quantise("xq1a", gx0, half), 0, half)
-        gx1 = woven("vector", xs[1][:, :, half:C], half, "tail2")
-        qz0 = quantise("zq1a", gz0, half)
-        qx1 = quantise("xq1b", gx1, half)
-        gz1 = woven("vector", zs[1][:, :, half:C], half, "tail3")
-        second_stage(1, "z", qz0, 0, half)
+        weave_pair("vector", xs[1], gx, 2, 0, half)
+        weave_pair("vector", xs[1], gx, 2, half, C)
+        quantise_into(qx1, gx, 0, half)
+        second_stage(1, "x", qx1, 0, half)
+        weave_pair("vector", zs[1], gz, 2, 0, half)
+        quantise_into(qx1, gx, half, C)
         second_stage(1, "x", qx1, half, C)
-        qz1 = quantise("zq1b", gz1, half)
-        second_stage(1, "z", qz1, half, C)
+        weave_pair("vector", zs[1], gz, 2, half, C)
+        quantise_into(qz1, gz, 0, half)
+        quantise_into(qz1, gz, half, C)
+        second_stage(1, "z", qz1)
         for n in range(NT):
-            result = keep.tile([P, C], F32, name="result", tag="raw%d" % n)
+            result = tile([P, C], F32, "result", "page%d%d" % slices[n])
             copy_on("scalar" if n % 2 == 0 else "vector", result[:], accs[n][:])
             nc.sync.dma_start(out=out[P * n : P * (n + 1), :], in_=result[:])

@@ -1,6 +1,7 @@
 from contextlib import ExitStack
 
 import concourse.mybir as mybir
+from concourse.masks import make_identity
 
 K, H, N, T, S, T2, C = 1024, 1024, 768, 2048, 512, 1024, 512
 FLOPS = 2 * (2 * K * H * S + 2 * H * N * C)
@@ -40,16 +41,16 @@ def tile_list_cart_board_completion_kernel(
             return keep.tile(shape, dtype, name=name, tag=slot or name, align_bytes=64)
 
         def cleared(name, width):
-            plane = tile([P, width], U8, name)
-            nc.vector.memset(plane[:].bitcast(I32), 0)
+            plane = tile([P, KP, width], U8, name)
+            nc.vector.memset(plane[:].rearrange("p a c -> p (a c)").bitcast(I32), 0)
             return plane
 
         def load_scales(plane, src):
             for q in range(QUADS):
-                nc.scalar.dma_start(out=plane[32 * q : 32 * q + 8, :].bitcast(I32), in_=src[:, 4 * q : 4 * q + 4, :].bitcast(I32))
-
-        def second_plane(packed, shifted):
-            nc.gpsimd.dma_start(out=shifted[0 : P - 4, :].bitcast(I32), in_=packed[4:P, :].bitcast(I32))
+                nc.sync.dma_start(
+                    out=plane[32 * q : 32 * q + 4].bitcast(I32),
+                    in_=src[:, 4 * q : 4 * q + 4, :].rearrange("a r c -> r a c").bitcast(I32),
+                )
 
         def raw_rows(src, a, c0, width, slot):
             raw = tile([P, PACK, width], F32, "raw", slot)
@@ -82,43 +83,34 @@ def tile_list_cart_board_completion_kernel(
             weave(engine, rows, grouped[:])
             return grouped
 
-        def woven_w1(engine, raw, slot):
+        def woven_w1(split, raw, slot):
             grouped = tile([P, PASS * PACK], BF16, "grouped", slot)
-            copy_on(
-                engine,
-                grouped[:].rearrange("p (t m j) -> p m j t", t=PACK, j=PACK),
-                raw[:].rearrange("p j (m t) -> p m j t", t=PACK),
-            )
+            dst = grouped[:].rearrange("p (t m j) -> p m j t", t=PACK, j=PACK)
+            src = raw[:].rearrange("p j (m t) -> p m j t", t=PACK)
+            if split > 0:
+                nc.vector.tensor_copy(out=dst[:, :split], in_=src[:, :split])
+            if split < P:
+                nc.scalar.copy(out=dst[:, split:], in_=src[:, split:])
             return grouped
 
-        w2_plane_raw = cleared("w2_plane_raw", H)
         tab_plane = cleared("tab_plane", T)
-        w2_shifted = cleared("w2_shifted", H)
-        v_shifted = cleared("v_shifted", S)
+        w2_plane_raw = cleared("w2_plane_raw", H)
         w4_plane = cleared("w4_plane", N)
         list1 = keep.tile([P, S // 16], U16, name="list1")
         nc.sync.dma_start(list1[:], offs)
         w2_raw = tile([P, KP, 2 * H], U8, "w2_raw")
         nc.sync.dma_start(out=w2_raw[:].bitcast(I32), in_=w2_words.rearrange("a p c -> p a c").bitcast(I32))
-        load_scales(w2_plane_raw, w2_scales)
         load_scales(tab_plane, tab_scales)
-        load_scales(w4_plane, w4_scales)
-        w1_raw = {}
+        wgs_raw = tile([P, S], F32, "wgs_raw")
+        nc.sync.dma_start(out=wgs_raw[:], in_=wgs)
+        w1_raw = {(0, 0): raw_rows(w1, 0, 0, PASS, "raw0")}
+        load_scales(w2_plane_raw, w2_scales)
+        w1_raw[1, 0] = raw_rows(w1, 1, 0, PASS, "raw1")
+        tab_sb = [tile([P, T], I32, "tab%d" % a) for a in range(KP)]
         for a in range(KP):
-            w1_raw[a, 0] = raw_rows(w1, a, 0, PASS, "raw%d" % a)
-        tab_sb = []
-        for a in range(KP):
-            words = tile([P, T], I32, "tab%d" % a)
-            nc.sync.dma_start(out=words[:], in_=tab_words[a].rearrange("p t i -> p (t i)").bitcast(I32))
-            tab_sb.append(words)
+            nc.sync.dma_start(out=tab_sb[a][:], in_=tab_words[a].rearrange("p t i -> p (t i)").bitcast(I32))
         list2 = keep.tile([P, S // 16], U16, name="list2")
         nc.sync.dma_start(list2[:], offs2)
-        list3 = keep.tile([P, C // 16], U16, name="list3")
-        nc.sync.dma_start(list3[:], offs3)
-        wgs_rows = wgs.rearrange("(q t) s -> q t s", t=PACK)
-        wgs_first = tile([P, 1, S], F32, "wgs_first")
-        for q in range(QUADS):
-            nc.sync.dma_start(out=wgs_first[32 * q : 32 * q + 32], in_=wgs_rows[:, 0:1, :])
         pages = {}
 
         def load_page(b, t):
@@ -131,13 +123,15 @@ def tile_list_cart_board_completion_kernel(
             w3_raw[b, c0] = raw_rows(w3, b, c0, min(PASS, N - c0), ("raw_narrow%d" % b) if c0 else "raw%d" % (4 + b))
 
         load_page(0, 0)
-        load_page(0, 1)
+        list3 = keep.tile([P, C // 16], U16, name="list3")
+        nc.sync.dma_start(list3[:], offs3)
         sharp_sb = tile([P, HP, PACK], F32, "sharp_sb")
         gain_sb = tile([P, HP, PACK], F32, "gain_sb")
         nc.sync.dma_start(out=sharp_sb[:], in_=sharp.rearrange("(b p t) -> p b t", b=HP, t=PACK))
         nc.sync.dma_start(out=gain_sb[:], in_=gain.rearrange("(b p t) -> p b t", b=HP, t=PACK))
         w1_raw[0, 1] = raw_rows(w1, 0, PASS, PASS, "raw2")
         w1_raw[1, 1] = raw_rows(w1, 1, PASS, PASS, "raw3")
+        load_page(0, 1)
         load_w3(0, 0)
         load_page(0, 2)
         load_w3(0, PASS)
@@ -146,21 +140,41 @@ def tile_list_cart_board_completion_kernel(
         load_page(1, 0)
         load_w3(1, PASS)
         load_page(1, 1)
+        load_scales(w4_plane, w4_scales)
         w4_sb = tile([P, HP, N], I32, "w4_sb")
         nc.sync.dma_start(out=w4_sb[:], in_=w4_words.rearrange("a p c i -> p a (c i)").bitcast(I32))
         load_page(1, 2)
         load_page(1, 3)
 
-        w2_sb = tile([P, KP * HP, 2 * PASS], U8, "w2_sb")
-        w2_plane = tile([P, H], U8, "w2_plane")
-        nc.vector.tensor_copy(
-            out=w2_plane[:].rearrange("p (b t m) -> p b m t", b=HP, t=PACK),
-            in_=w2_plane_raw[:].rearrange("p (b m t) -> p b m t", b=HP, t=PACK),
+        identity = tile([P, P], F32, "identity")
+        make_identity(nc, identity[:])
+        turned = psum.tile([P, S // P, P], F32, name="turned", tag="bank0")
+        for c in range(S // P):
+            nc.tensor.transpose(turned[:, c, :], wgs_raw[:, P * c : P * (c + 1)], identity[:])
+        spread = tile([P, S // P, PACK, QUADS, 32], F32, "spread", "xs0")
+        nc.scalar.copy(
+            out=spread[:],
+            in_=turned[:].rearrange("j c (q t) -> j c t q", t=PACK).unsqueeze(3).to_broadcast([P, S // P, PACK, QUADS, 32]),
         )
-        second_plane(w2_plane, w2_shifted)
-        v_plane = tile([P, S], U8, "v_plane")
-        nc.vector.tensor_copy(v_plane[:], tab_plane[:].indirect(list1[:]))
-        second_plane(v_plane, v_shifted)
+        w1_grouped = [woven_w1(0, w1_raw[a, 0], "grouped%d" % a) for a in range(KP)]
+        wgs_first = tile([P, S], F32, "wgs_first", "raw0")
+        wgs_rest = tile([P, PACK - 1, S], F32, "wgs_rest", "raw1")
+        wgs_sb = [wgs_first[:]] + [wgs_rest[:, t] for t in range(PACK - 1)]
+        for t in range(PACK):
+            back = psum.tile([P, S // P, P], F32, name="back", tag="bank%d" % (2 + t))
+            for c in range(S // P):
+                nc.tensor.transpose(back[:, c, :], spread[:, c, t].rearrange("j g q -> j (g q)"), identity[:])
+            nc.scalar.copy(out=wgs_sb[t], in_=back[:].rearrange("p c j -> p (c j)"))
+
+        w2_sb = tile([P, KP * HP, 2 * PASS], U8, "w2_sb")
+        w2_plane = tile([P, KP * HP, PASS], U8, "w2_plane")
+        nc.vector.tensor_copy(
+            out=w2_plane[:].rearrange("p g (t m) -> p g m t", t=PACK),
+            in_=w2_plane_raw[:].rearrange("p a (b m t) -> p (a b) m t", b=HP, t=PACK),
+        )
+        v_planes = [tile([P, S], U8, "v_plane%d" % a) for a in range(KP)]
+        for a in range(KP):
+            nc.vector.tensor_copy(v_planes[a][:], tab_plane[:, a, :].indirect(list1[:]))
         nc.vector.tensor_copy(
             out=w2_sb[:].bitcast(U16).rearrange("p g (t m) -> p g m t", t=PACK),
             in_=w2_raw[:].bitcast(U16).rearrange("p a (b m t) -> p (a b) m t", b=HP, t=PACK),
@@ -181,59 +195,48 @@ def tile_list_cart_board_completion_kernel(
             weave("scalar", raw[:], w3_grouped[b][:, PACK * c0 : PACK * (c0 + raw.shape[2])])
 
         slices = [(b, t) for b in range(HP) for t in range(PACK)]
-        contents_slot = {}
-        bent_slot = {i: contents_slot.get(i + 2, "contents%d" % (i + 2)) for i in range(6)}
+        bent_slot = {0: "raw2"}
+        affinity_slot = {3: "raw3", len(slices) - 1: "zs0"}
 
-        def first_stage(i):
+        def stage_one_pass(acc, lhs, lhs_scale, a):
+            nc.tensor.matmul_mx(
+                out=acc[:],
+                lhsT=lhs,
+                lhsT_scale=lhs_scale,
+                rhs=v_codes[a][:].bitcast(FP8X4),
+                rhs_scale=v_planes[a][:],
+                start=(a == 0),
+                stop=(a == KP - 1),
+            )
+
+        def affinity_of(i):
             b, t = slices[i]
-            cols = slice(P * t, P * (t + 1))
-            wide = slice(PASS * b + P * t, PASS * b + P * (t + 1))
-            acc_a = psum.tile([P, S], F32, name="acc_a", tag="acc_a")
-            acc_b = psum.tile([P, S], F32, name="acc_b", tag="acc_b")
-            passes = [(name, a) for a in range(KP) for name in "ab"] if i == 0 else [(name, a) for name in "ba" for a in range(KP)]
-            for name, a in passes:
-                if name == "a":
-                    acc, lhs, lhs_scale = acc_a, w1_q[a, b][0][:, cols].bitcast(FP8X4), w1_q[a, b][1][:, cols]
-                    rhs_scale = v_plane[4 * a : P, :]
-                else:
-                    acc, lhs = acc_b, w2_sb[:, a * HP + b, 2 * P * t : 2 * P * (t + 1)].bitcast(FP4X4)
-                    lhs_scale, rhs_scale = (w2_plane, w2_shifted)[a][:, wide], (v_plane, v_shifted)[a][:]
-                nc.tensor.matmul_mx(
-                    out=acc[:],
-                    lhsT=lhs,
-                    lhsT_scale=lhs_scale,
-                    rhs=v_codes[a][:].bitcast(FP8X4),
-                    rhs_scale=rhs_scale,
-                    start=(a == 0),
-                    stop=(a == KP - 1),
-                )
-            wgs_t = wgs_first[:, 0, :] if t == 0 else wgs_rest[:, t - 1, :]
-            weighted = ring.tile([P, S], F32, name="weighted", bufs=3)
-            if i == 0:
-                put = tile([P, S], F32, "put0")
-                nc.vector.tensor_tensor(weighted[:], acc_a[:], wgs_t, MULT)
-                nc.vector.tensor_tensor(put[:], acc_b[:], weighted[:], MULT)
-                return put
-            contents = tile([P, S], F32, "contents", contents_slot.get(i, "contents%d" % i))
-            nc.scalar.copy(out=contents[:], in_=acc_a[:])
-            affinity = tile([P, S], F32, "affinity%d" % i)
-            nc.scalar.copy(out=affinity[:], in_=acc_b[:])
-            nc.gpsimd.tensor_tensor(weighted[:], contents[:], wgs_t, MULT)
-            return weighted, affinity
+            acc = psum.tile([P, S], F32, name="acc_b", tag="bank7")
+            for a in range(KP):
+                g = a * HP + b
+                stage_one_pass(acc, w2_sb[:, g, 2 * P * t : 2 * P * (t + 1)].bitcast(FP4X4), w2_plane[:, g, P * t : P * (t + 1)], a)
+            affinity = tile([P, S], F32, "affinity", affinity_slot.get(i, "affinity%d" % i))
+            nc.scalar.copy(out=affinity[:], in_=acc[:])
+            return affinity
 
-        def product(i, weighted, contents):
-            put = tile([P, S], F32, "put", "zs0" if i == last else "put%d" % (i % 2))
-            nc.gpsimd.tensor_tensor(put[:], weighted[:], contents[:], MULT)
-            return put
+        def weighted_of(i):
+            b, t = slices[i]
+            acc = psum.tile([P, S], F32, name="acc_a", tag="bank6")
+            for a in range(KP):
+                codes, scales = w1_q[a, b]
+                stage_one_pass(acc, codes[:, P * t : P * (t + 1)].bitcast(FP8X4), scales[:, P * t : P * (t + 1)], a)
+            weighted = tile([P, S], F32, "weighted")
+            nc.vector.tensor_tensor(weighted[:], acc[:], wgs_sb[t], MULT)
+            return weighted
 
-        accs = [psum.tile([P, C], F32, name="out%d" % n, tag="out%d" % n) for n in range(NT)]
+        accs = []
 
         def second_stage(b, which, moving, c_lo=0, c_hi=C):
             codes, scales = moving
             for n in range(NT):
                 cols = slice(P * n, P * (n + 1))
                 if which == "x":
-                    lhs, lhs_scale = w4_sb[:, b, cols], w4_plane[4 * b : P, cols]
+                    lhs, lhs_scale = w4_sb[:, b, cols], w4_plane[:, b, cols]
                 else:
                     c0 = P * n // PASS * PASS
                     lhs, lhs_scale = (part[:, P * n - c0 : P * (n + 1) - c0] for part in w3_q[b, c0])
@@ -247,29 +250,26 @@ def tile_list_cart_board_completion_kernel(
                     stop=(b == HP - 1 and which == "z" and c_hi == C),
                 )
 
-        w1_q[0, 0] = quantise("w1q00", woven_w1("vector", w1_raw[0, 0], "grouped0"), PASS)
-        grouped = woven_w1("scalar", w1_raw[1, 0], "grouped1")
+        w1_q[0, 0] = quantise("w1q00", w1_grouped[0], PASS, "w2_plane_raw")
         gather_words(0)
-        wgs_rest = tile([P, PACK - 1, S], F32, "wgs_rest", "tab0")
-        for q in range(QUADS):
-            nc.scalar.dma_start(out=wgs_rest[32 * q : 32 * q + 32], in_=wgs_rows[:, 1:PACK, :])
-        w1_q[1, 0] = quantise("w1q10", grouped, PASS)
+        w1_q[1, 0] = quantise("w1q10", w1_grouped[1], PASS, "tab0")
         gather_words(1)
 
-        xs = [tile([P, PACK, C], F32, "xs0"), tile([P, PACK, C], F32, "xs1", "raw0")]
+        xs = [tile([P, PACK, C], F32, "xs0"), tile([P, PACK, C], F32, "xs1", "tab1")]
         zs = [tile([P, PACK, C], BF16, "zs0"), tile([P, PACK, C], BF16, "zs1", "w2_raw")]
         half = C // 2
         last = len(slices) - 1
 
+        bents = {}
+
         def read_page(i, lo, hi):
             b, t = slices[i]
             nc.vector.tensor_copy(xs[b][:, t, lo:hi], pages[b, t][:].indirect(list3[:, lo // 16 : hi // 16]))
-            bent = tile([P, hi - lo], F32, "bent", bent_slot.get(i, "bent%d" % (i % 2 + lo // half)))
-            nc.scalar.activation(out=bent[:], in_=xs[b][:, t, lo:hi], func=TANH, scale=sharp_sb[:, b, t : t + 1])
-            if i == last:
-                nc.scalar.activation(out=zs[b][:, t, lo:hi], in_=bent[:], func=COPY, scale=gain_sb[:, b, t : t + 1])
-            else:
-                nc.gpsimd.tensor_scalar(zs[b][:, t, lo:hi], bent[:], gain_sb[:, b, t : t + 1], 0.0, MULT, ADD)
+            if lo == 0:
+                bents[i] = tile([P, C], F32, "bent", bent_slot.get(i, "bent"))
+            bent = bents[i][:, lo:hi]
+            nc.scalar.activation(out=bent, in_=xs[b][:, t, lo:hi], func=TANH, scale=sharp_sb[:, b, t : t + 1])
+            nc.scalar.activation(out=zs[b][:, t, lo:hi], in_=bent, func=COPY, scale=gain_sb[:, b, t : t + 1])
 
         def codes_slot(i):
             return "affinity%d" % i
@@ -285,21 +285,21 @@ def tile_list_cart_board_completion_kernel(
             codes, scales = target
             nc.vector.quantize_mx(out=codes[:, lo:hi].bitcast(FP8X4), scales=scales[:, lo:hi], in_=grouped[:, PACK * lo : PACK * hi])
 
-        puts = {0: first_stage(0), 1: product(1, *first_stage(1))}
-        parts = {}
+        weighted = weighted_of(0)
+        affinities = {0: affinity_of(0), 1: affinity_of(1)}
         weave_at = {0: (0, 1), 2: (2,), 3: (3,)}
         w3_pieces = [(0, 0), (0, PASS), (1, 0), (1, PASS)]
-        products_after = {0: (2,), 1: (3, 4), 2: (5,), 3: (6, 7)}
+
         grouped = {}
-        gx = tile([P, C * PACK], BF16, "gx", "raw1")
-        gz = tile([P, C * PACK], BF16, "gz", "tab1")
+        gx = tile([P, C * PACK], BF16, "gx", "wgs_raw")
+        gz = tile([P, C * PACK], BF16, "gz", "w2_sb_spare")
         for i, (b, t) in enumerate(slices):
-            nc.vector.tensor_copy(pages[b, t][:].indirect(list2[:]), puts[i][:])
+            nc.vector.tensor_tensor(pages[b, t][:].indirect(list2[:]), weighted[:], affinities[i][:], MULT)
             if i == last:
                 break
             if i == 0:
-                grouped["w1a"] = woven_w1("scalar", w1_raw[0, 1], "grouped0")
-                grouped["w1b"] = woven_w1("scalar", w1_raw[1, 1], "grouped1")
+                grouped["w1a"] = woven_w1(0, w1_raw[0, 1], "grouped0")
+                grouped["w1b"] = woven_w1(0, w1_raw[1, 1], "grouped1")
             if i == 1:
                 codes = tile([P, KP * PASS], U32, "w1q_codes", codes_slot(i))
                 scales = tile([P, KP * PASS], U8, "w1q_scales")
@@ -311,13 +311,12 @@ def tile_list_cart_board_completion_kernel(
             if 2 <= i <= 5:
                 wb, c0 = w3_pieces[i - 2]
                 width = w3_raw[wb, c0].shape[2]
-                w3_q[wb, c0] = quantise("w3q%d" % i, w3_grouped[wb][:, PACK * c0 : PACK * (c0 + width)], width, codes_slot(i))
+                w3_q[wb, c0] = quantise("w3q%d" % i, w3_grouped[wb][:, PACK * c0 : PACK * (c0 + width)], width)
             if i == 6:
-                qx0 = quantise("xq0", grouped["x"], C, codes_slot(i))
-            for ahead in products_after.get(i, ()):
-                parts[ahead] = first_stage(ahead)
+                qx0 = quantise("xq0", grouped["x"], C)
+            weighted = weighted_of(i + 1)
             if i + 2 <= last:
-                puts[i + 2] = product(i + 2, *parts[i + 2])
+                affinities[i + 2] = affinity_of(i + 2)
             read_page(i, 0, C)
             if i == 3:
                 grouped["x"] = woven("scalar", xs[0][:], C, "grouped0")
@@ -326,7 +325,8 @@ def tile_list_cart_board_completion_kernel(
                 weave_pair("scalar", xs[1], gx, 0, 0, C)
                 weave_pair("scalar", zs[1], gz, 0, 0, C)
             if i == 6:
-                z_codes = tile([P, C], U32, "z_codes", "put0")
+                accs.extend(psum.tile([P, C], F32, name="out%d" % n, tag="bank%d" % n) for n in range(NT))
+                z_codes = tile([P, C], U32, "z_codes", "affinity6")
                 z_scales = tile([P, C], U8, "zq0_scales")
                 quantise_into((z_codes, z_scales), grouped["z"], 0, C)
                 second_stage(0, "z", (z_codes, z_scales))

@@ -211,7 +211,7 @@ def tile_list_cart_board_completion_kernel(
 
         def affinity_of(i):
             b, t = slices[i]
-            acc = psum.tile([P, S], F32, name="acc_b", tag="bank7")
+            acc = psum.tile([P, S], F32, name="acc_b", tag="bank1" if i == 1 else "bank7")
             for a in range(KP):
                 g = a * HP + b
                 stage_one_pass(acc, w2_sb[:, g, 2 * P * t : 2 * P * (t + 1)].bitcast(FP4X4), w2_plane[:, g, P * t : P * (t + 1)], a)
@@ -221,13 +221,22 @@ def tile_list_cart_board_completion_kernel(
 
         def weighted_of(i):
             b, t = slices[i]
-            acc = psum.tile([P, S], F32, name="acc_a", tag="bank6")
+            acc = psum.tile([P, S], F32, name="acc_a", tag="bank0" if i == 1 else "bank6")
             for a in range(KP):
                 codes, scales = w1_q[a, b]
                 stage_one_pass(acc, codes[:, P * t : P * (t + 1)].bitcast(FP8X4), scales[:, P * t : P * (t + 1)], a)
-            weighted = tile([P, S], F32, "weighted")
-            nc.vector.tensor_tensor(weighted[:], acc[:], wgs_sb[t], MULT)
-            return weighted
+            if i <= 1:
+                weighted = tile([P, S], F32, "weighted", "weighted%d" % i)
+                nc.vector.tensor_tensor(weighted[:], acc[:], wgs_sb[t], MULT)
+                return weighted
+            contents = tile([P, S], F32, "contents", "contents%d" % (i % 3))
+            nc.scalar.copy(out=contents[:], in_=acc[:])
+            return contents
+
+        def put_of(i, contents, affinity):
+            weighted = tile([P, S], F32, "weighted", "weighted%d" % (i % 2))
+            nc.gpsimd.tensor_tensor(weighted[:], contents[:], wgs_sb[slices[i][1]], MULT)
+            return weighted, affinity
 
         accs = []
 
@@ -286,38 +295,44 @@ def tile_list_cart_board_completion_kernel(
             nc.vector.quantize_mx(out=codes[:, lo:hi].bitcast(FP8X4), scales=scales[:, lo:hi], in_=grouped[:, PACK * lo : PACK * hi])
 
         weighted = weighted_of(0)
-        affinities = {0: affinity_of(0), 1: affinity_of(1)}
-        weave_at = {0: (0, 1), 2: (2,), 3: (3,)}
+        puts = {0: (weighted, affinity_of(0))}
+        puts[1] = weighted_of(1), affinity_of(1)
+        weave_at = {1: (0,), 2: (1, 2), 3: (3,)}
         w3_pieces = [(0, 0), (0, PASS), (1, 0), (1, PASS)]
 
+        contents = {2: weighted_of(2)}
+        affinities = {}
         grouped = {}
         gx = tile([P, C * PACK], BF16, "gx", "wgs_raw")
         gz = tile([P, C * PACK], BF16, "gz", "w2_sb_spare")
         for i, (b, t) in enumerate(slices):
-            nc.vector.tensor_tensor(pages[b, t][:].indirect(list2[:]), weighted[:], affinities[i][:], MULT)
+            nc.vector.tensor_tensor(pages[b, t][:].indirect(list2[:]), puts[i][0][:], puts[i][1][:], MULT)
             if i == last:
                 break
             if i == 0:
                 grouped["w1a"] = woven_w1(0, w1_raw[0, 1], "grouped0")
                 grouped["w1b"] = woven_w1(0, w1_raw[1, 1], "grouped1")
             if i == 1:
-                codes = tile([P, KP * PASS], U32, "w1q_codes", codes_slot(i))
+                codes = tile([P, KP * PASS], U32, "w1q_codes", "affinity1")
                 scales = tile([P, KP * PASS], U8, "w1q_scales")
                 for a, name in enumerate(("w1a", "w1b")):
                     w1_q[a, 1] = codes[:, PASS * a : PASS * (a + 1)], scales[:, PASS * a : PASS * (a + 1)]
                     quantise_into(w1_q[a, 1], grouped[name], 0, PASS)
-            for piece in weave_at.get(i, ()):
-                weave_w3(*w3_pieces[piece])
             if 2 <= i <= 5:
                 wb, c0 = w3_pieces[i - 2]
                 width = w3_raw[wb, c0].shape[2]
                 w3_q[wb, c0] = quantise("w3q%d" % i, w3_grouped[wb][:, PACK * c0 : PACK * (c0 + width)], width)
             if i == 6:
                 qx0 = quantise("xq0", grouped["x"], C)
-            weighted = weighted_of(i + 1)
             if i + 2 <= last:
                 affinities[i + 2] = affinity_of(i + 2)
+            if i + 3 <= last:
+                contents[i + 3] = weighted_of(i + 3)
+            for piece in weave_at.get(i, ()):
+                weave_w3(*w3_pieces[piece])
             read_page(i, 0, C)
+            if i + 2 <= last:
+                puts[i + 2] = put_of(i + 2, contents[i + 2], affinities[i + 2])
             if i == 3:
                 grouped["x"] = woven("scalar", xs[0][:], C, "grouped0")
                 grouped["z"] = woven("scalar", zs[0][:], C, "grouped1")

from contextlib import ExitStack

import concourse.mybir as mybir
from concourse.masks import make_identity

K, H, N, T, S, T2, C = 1024, 1024, 768, 2048, 512, 1024, 512
FLOPS = 2 * (2 * K * H * S + 2 * H * N * C)

F32 = mybir.dt.float32
BF16 = mybir.dt.bfloat16
I32 = mybir.dt.int32
U32 = mybir.dt.uint32
U16 = mybir.dt.uint16
U8 = mybir.dt.uint8
FP8X4 = mybir.dt.float8_e4m3fn_x4
FP4X4 = mybir.dt.float4_e2m1fn_x4
MULT = mybir.AluOpType.mult
ADD = mybir.AluOpType.add
TANH = mybir.ActivationFunctionType.Tanh
COPY = mybir.ActivationFunctionType.Copy

P = 128
PACK = 4
PASS = P * PACK
KP = K // PASS
HP = H // PASS
NT = N // P
QUADS = 4


def tile_list_cart_board_completion_kernel(
    tc, tab_words, tab_scales, offs, offs2, offs3, w1, w2_words, w2_scales, wgs, page0, sharp, gain, w3, w4_words, w4_scales, out
):
    nc = tc.nc
    with ExitStack() as ctx:
        keep = ctx.enter_context(tc.tile_pool(name="keep", bufs=1))
        ring = ctx.enter_context(tc.tile_pool(name="ring", bufs=2))
        psum = ctx.enter_context(tc.psum_pool(name="psum", bufs=1))

        def tile(shape, dtype, name, slot=None):
            return keep.tile(shape, dtype, name=name, tag=slot or name, align_bytes=64)

        def cleared(name, width):
            plane = tile([P, KP, width], U8, name)
            nc.vector.memset(plane[:].rearrange("p a c -> p (a c)").bitcast(I32), 0)
            return plane

        def load_scales(plane, src):
            for q in range(QUADS):
                nc.sync.dma_start(
                    out=plane[32 * q : 32 * q + 4].bitcast(I32),
                    in_=src[:, 4 * q : 4 * q + 4, :].rearrange("a r c -> r a c").bitcast(I32),
                )

        def raw_rows(src, a, c0, width, slot):
            raw = tile([P, PACK, width], F32, "raw", slot)
            nc.sync.dma_start(out=raw[:], in_=src[PASS * a : PASS * (a + 1), c0 : c0 + width].rearrange("(p j) c -> p j c", j=PACK))
            return raw

        def quantise(name, grouped, width, slot=None):
            codes = tile([P, width], U32, name + "_codes", slot)
            scales = tile([P, width], U8, name + "_scales")
            for lo in range(0, width, PASS):
                hi = min(lo + PASS, width)
                nc.vector.quantize_mx(out=codes[:, lo:hi].bitcast(FP8X4), scales=scales[:, lo:hi], in_=grouped[:, PACK * lo : PACK * hi])
            return codes, scales

        def copy_on(engine, out, in_):
            if engine == "scalar":
                nc.scalar.copy(out=out, in_=in_)
            else:
                nc.vector.tensor_copy(out=out, in_=in_)

        def weave(engine, rows, grouped):
            copy_on(
                engine,
                grouped.rearrange("p (c i j) -> p c j i", i=4, j=PACK),
                rows.rearrange("p j (c i) -> p c j i", i=4),
            )

        def woven(engine, rows, width, slot):
            grouped = tile([P, width * PACK], BF16, "grouped", slot)
            weave(engine, rows, grouped[:])
            return grouped

        def woven_w1(split, raw, slot):
            grouped = tile([P, PASS * PACK], BF16, "grouped", slot)
            dst = grouped[:].rearrange("p (t m j) -> p m j t", t=PACK, j=PACK)
            src = raw[:].rearrange("p j (m t) -> p m j t", t=PACK)
            if split > 0:
                nc.vector.tensor_copy(out=dst[:, :split], in_=src[:, :split])
            if split < P:
                nc.scalar.copy(out=dst[:, split:], in_=src[:, split:])
            return grouped

        tab_plane = cleared("tab_plane", T)
        w2_plane_raw = cleared("w2_plane_raw", H)
        w4_plane = cleared("w4_plane", N)
        list1 = keep.tile([P, S // 16], U16, name="list1")
        nc.sync.dma_start(list1[:], offs)
        w2_raw = tile([P, KP, 2 * H], U8, "w2_raw")
        nc.sync.dma_start(out=w2_raw[:].bitcast(I32), in_=w2_words.rearrange("a p c -> p a c").bitcast(I32))
        load_scales(tab_plane, tab_scales)
        wgs_raw = tile([P, S], F32, "wgs_raw")
        nc.sync.dma_start(out=wgs_raw[:], in_=wgs)
        w1_raw = {(0, 0): raw_rows(w1, 0, 0, PASS, "raw0")}
        load_scales(w2_plane_raw, w2_scales)
        w1_raw[1, 0] = raw_rows(w1, 1, 0, PASS, "raw1")
        tab_sb = [tile([P, T], I32, "tab%d" % a) for a in range(KP)]
        for a in range(KP):
            nc.sync.dma_start(out=tab_sb[a][:], in_=tab_words[a].rearrange("p t i -> p (t i)").bitcast(I32))
        list2 = keep.tile([P, S // 16], U16, name="list2")
        nc.sync.dma_start(list2[:], offs2)
        pages = {}

        def load_page(b, t):
            pages[b, t] = tile([P, T2], F32, "page%d%d" % (b, t))
            nc.sync.dma_start(out=pages[b, t][:], in_=page0[PASS * b : PASS * (b + 1), :].rearrange("(p t) c -> p t c", t=PACK)[:, t, :])

        w3_raw = {}

        def load_w3(b, c0):
            w3_raw[b, c0] = raw_rows(w3, b, c0, min(PASS, N - c0), ("raw_narrow%d" % b) if c0 else "raw%d" % (4 + b))

        load_page(0, 0)
        list3 = keep.tile([P, C // 16], U16, name="list3")
        nc.sync.dma_start(list3[:], offs3)
        sharp_sb = tile([P, HP, PACK], F32, "sharp_sb")
        gain_sb = tile([P, HP, PACK], F32, "gain_sb")
        nc.sync.dma_start(out=sharp_sb[:], in_=sharp.rearrange("(b p t) -> p b t", b=HP, t=PACK))
        nc.sync.dma_start(out=gain_sb[:], in_=gain.rearrange("(b p t) -> p b t", b=HP, t=PACK))
        w1_raw[0, 1] = raw_rows(w1, 0, PASS, PASS, "raw2")
        w1_raw[1, 1] = raw_rows(w1, 1, PASS, PASS, "raw3")
        load_page(0, 1)
        load_w3(0, 0)
        load_page(0, 2)
        load_w3(0, PASS)
        load_page(0, 3)
        load_w3(1, 0)
        load_page(1, 0)
        load_w3(1, PASS)
        load_page(1, 1)
        load_scales(w4_plane, w4_scales)
        w4_sb = tile([P, HP, N], I32, "w4_sb")
        nc.sync.dma_start(out=w4_sb[:], in_=w4_words.rearrange("a p c i -> p a (c i)").bitcast(I32))
        load_page(1, 2)
        load_page(1, 3)

        identity = tile([P, P], F32, "identity")
        make_identity(nc, identity[:])
        turned = psum.tile([P, S // P, P], F32, name="turned", tag="bank0")
        for c in range(S // P):
            nc.tensor.transpose(turned[:, c, :], wgs_raw[:, P * c : P * (c + 1)], identity[:])
        spread = tile([P, S // P, PACK, QUADS, 32], F32, "spread", "xs0")
        nc.scalar.copy(
            out=spread[:],
            in_=turned[:].rearrange("j c (q t) -> j c t q", t=PACK).unsqueeze(3).to_broadcast([P, S // P, PACK, QUADS, 32]),
        )
        w1_grouped = [woven_w1(0, w1_raw[a, 0], "grouped%d" % a) for a in range(KP)]
        wgs_first = tile([P, S], F32, "wgs_first", "raw0")
        wgs_rest = tile([P, PACK - 1, S], F32, "wgs_rest", "raw1")
        wgs_sb = [wgs_first[:]] + [wgs_rest[:, t] for t in range(PACK - 1)]
        for t in range(PACK):
            back = psum.tile([P, S // P, P], F32, name="back", tag="bank%d" % (2 + t))
            for c in range(S // P):
                nc.tensor.transpose(back[:, c, :], spread[:, c, t].rearrange("j g q -> j (g q)"), identity[:])
            nc.scalar.copy(out=wgs_sb[t], in_=back[:].rearrange("p c j -> p (c j)"))

        w2_sb = tile([P, KP * HP, 2 * PASS], U8, "w2_sb")
        w2_plane = tile([P, KP * HP, PASS], U8, "w2_plane")
        nc.vector.tensor_copy(
            out=w2_plane[:].rearrange("p g (t m) -> p g m t", t=PACK),
            in_=w2_plane_raw[:].rearrange("p a (b m t) -> p (a b) m t", b=HP, t=PACK),
        )
        v_planes = [tile([P, S], U8, "v_plane%d" % a) for a in range(KP)]
        for a in range(KP):
            nc.vector.tensor_copy(v_planes[a][:], tab_plane[:, a, :].indirect(list1[:]))
        nc.vector.tensor_copy(
            out=w2_sb[:].bitcast(U16).rearrange("p g (t m) -> p g m t", t=PACK),
            in_=w2_raw[:].bitcast(U16).rearrange("p a (b m t) -> p (a b) m t", b=HP, t=PACK),
        )
        v_codes = []

        def gather_words(a):
            codes = tile([P, S], I32, "v_codes%d" % a)
            nc.vector.tensor_copy(codes[:].bitcast(U32), tab_sb[a][:].bitcast(U32).indirect(list1[:]))
            v_codes.append(codes)

        w1_q = {}
        w3_q = {}
        w3_grouped = [tile([P, N * PACK], BF16, "grouped_w3%d" % b) for b in range(HP)]

        def weave_w3(b, c0):
            raw = w3_raw[b, c0]
            weave("scalar", raw[:], w3_grouped[b][:, PACK * c0 : PACK * (c0 + raw.shape[2])])

        slices = [(b, t) for b in range(HP) for t in range(PACK)]
        bent_slot = {0: "raw2"}
        affinity_slot = {3: "raw3", len(slices) - 1: "zs0"}

        def stage_one_pass(acc, lhs, lhs_scale, a):
            nc.tensor.matmul_mx(
                out=acc[:],
                lhsT=lhs,
                lhsT_scale=lhs_scale,
                rhs=v_codes[a][:].bitcast(FP8X4),
                rhs_scale=v_planes[a][:],
                start=(a == 0),
                stop=(a == KP - 1),
            )

        def affinity_of(i):
            b, t = slices[i]
            acc = psum.tile([P, S], F32, name="acc_b", tag="bank1" if i == 1 else "bank7")
            for a in range(KP):
                g = a * HP + b
                stage_one_pass(acc, w2_sb[:, g, 2 * P * t : 2 * P * (t + 1)].bitcast(FP4X4), w2_plane[:, g, P * t : P * (t + 1)], a)
            affinity = tile([P, S], F32, "affinity", affinity_slot.get(i, "affinity%d" % i))
            nc.scalar.copy(out=affinity[:], in_=acc[:])
            return affinity

        def weighted_of(i):
            b, t = slices[i]
            acc = psum.tile([P, S], F32, name="acc_a", tag="bank0" if i == 1 else "bank6")
            for a in range(KP):
                codes, scales = w1_q[a, b]
                stage_one_pass(acc, codes[:, P * t : P * (t + 1)].bitcast(FP8X4), scales[:, P * t : P * (t + 1)], a)
            if i <= 1:
                weighted = tile([P, S], F32, "weighted", "weighted%d" % i)
                nc.vector.tensor_tensor(weighted[:], acc[:], wgs_sb[t], MULT)
                return weighted
            contents = tile([P, S], F32, "contents", "contents%d" % (i % 3))
            nc.scalar.copy(out=contents[:], in_=acc[:])
            return contents

        def put_of(i, contents, affinity):
            weighted = tile([P, S], F32, "weighted", "weighted%d" % (i % 2))
            nc.gpsimd.tensor_tensor(weighted[:], contents[:], wgs_sb[slices[i][1]], MULT)
            return weighted, affinity

        accs = []

        def second_stage(b, which, moving, c_lo=0, c_hi=C):
            codes, scales = moving
            for n in range(NT):
                cols = slice(P * n, P * (n + 1))
                if which == "x":
                    lhs, lhs_scale = w4_sb[:, b, cols], w4_plane[:, b, cols]
                else:
                    c0 = P * n // PASS * PASS
                    lhs, lhs_scale = (part[:, P * n - c0 : P * (n + 1) - c0] for part in w3_q[b, c0])
                nc.tensor.matmul_mx(
                    out=accs[n][:, c_lo:c_hi],
                    lhsT=lhs.bitcast(FP8X4),
                    lhsT_scale=lhs_scale,
                    rhs=codes[:, c_lo:c_hi].bitcast(FP8X4),
                    rhs_scale=scales[:, c_lo:c_hi],
                    start=(b == 0 and which == "z"),
                    stop=(b == HP - 1 and which == "z" and c_hi == C),
                )

        w1_q[0, 0] = quantise("w1q00", w1_grouped[0], PASS, "w2_plane_raw")
        gather_words(0)
        w1_q[1, 0] = quantise("w1q10", w1_grouped[1], PASS, "tab0")
        gather_words(1)

        xs = [tile([P, PACK, C], F32, "xs0"), tile([P, PACK, C], F32, "xs1", "tab1")]
        zs = [tile([P, PACK, C], BF16, "zs0"), tile([P, PACK, C], BF16, "zs1", "w2_raw")]
        half = C // 2
        last = len(slices) - 1

        bents = {}

        def read_page(i, lo, hi):
            b, t = slices[i]
            nc.vector.tensor_copy(xs[b][:, t, lo:hi], pages[b, t][:].indirect(list3[:, lo // 16 : hi // 16]))
            if lo == 0:
                bents[i] = tile([P, C], F32, "bent", bent_slot.get(i, "bent"))
            bent = bents[i][:, lo:hi]
            nc.scalar.activation(out=bent, in_=xs[b][:, t, lo:hi], func=TANH, scale=sharp_sb[:, b, t : t + 1])
            nc.scalar.activation(out=zs[b][:, t, lo:hi], in_=bent, func=COPY, scale=gain_sb[:, b, t : t + 1])

        def codes_slot(i):
            return "affinity%d" % i

        def weave_pair(engine, rows, grouped, j, lo, hi):
            copy_on(
                engine,
                grouped[:, PACK * lo : PACK * hi].rearrange("p (c i j) -> p c j i", i=4, j=PACK)[:, :, j : j + 2, :],
                rows[:, j : j + 2, lo:hi].rearrange("p j (c i) -> p c j i", i=4),
            )

        def quantise_into(target, grouped, lo, hi):
            codes, scales = target
            nc.vector.quantize_mx(out=codes[:, lo:hi].bitcast(FP8X4), scales=scales[:, lo:hi], in_=grouped[:, PACK * lo : PACK * hi])

        weighted = weighted_of(0)
        puts = {0: (weighted, affinity_of(0))}
        puts[1] = weighted_of(1), affinity_of(1)
        weave_at = {1: (0,), 2: (1, 2), 3: (3,)}
        w3_pieces = [(0, 0), (0, PASS), (1, 0), (1, PASS)]

        contents = {2: weighted_of(2)}
        affinities = {}
        grouped = {}
        gx = tile([P, C * PACK], BF16, "gx", "wgs_raw")
        gz = tile([P, C * PACK], BF16, "gz", "w2_sb_spare")
        for i, (b, t) in enumerate(slices):
            nc.vector.tensor_tensor(pages[b, t][:].indirect(list2[:]), puts[i][0][:], puts[i][1][:], MULT)
            if i == last:
                break
            if i == 0:
                grouped["w1a"] = woven_w1(0, w1_raw[0, 1], "grouped0")
                grouped["w1b"] = woven_w1(0, w1_raw[1, 1], "grouped1")
            if i == 1:
                codes = tile([P, KP * PASS], U32, "w1q_codes", "affinity1")
                scales = tile([P, KP * PASS], U8, "w1q_scales")
                for a, name in enumerate(("w1a", "w1b")):
                    w1_q[a, 1] = codes[:, PASS * a : PASS * (a + 1)], scales[:, PASS * a : PASS * (a + 1)]
                    quantise_into(w1_q[a, 1], grouped[name], 0, PASS)
            if 2 <= i <= 5:
                wb, c0 = w3_pieces[i - 2]
                width = w3_raw[wb, c0].shape[2]
                w3_q[wb, c0] = quantise("w3q%d" % i, w3_grouped[wb][:, PACK * c0 : PACK * (c0 + width)], width)
            if i == 6:
                qx0 = quantise("xq0", grouped["x"], C)
            if i + 2 <= last:
                affinities[i + 2] = affinity_of(i + 2)
            if i + 3 <= last:
                contents[i + 3] = weighted_of(i + 3)
            for piece in weave_at.get(i, ()):
                weave_w3(*w3_pieces[piece])
            read_page(i, 0, C)
            if i + 2 <= last:
                puts[i + 2] = put_of(i + 2, contents[i + 2], affinities[i + 2])
            if i == 3:
                grouped["x"] = woven("scalar", xs[0][:], C, "grouped0")
                grouped["z"] = woven("scalar", zs[0][:], C, "grouped1")
            if i == 5:
                weave_pair("scalar", xs[1], gx, 0, 0, C)
                weave_pair("scalar", zs[1], gz, 0, 0, C)
            if i == 6:
                accs.extend(psum.tile([P, C], F32, name="out%d" % n, tag="bank%d" % n) for n in range(NT))
                z_codes = tile([P, C], U32, "z_codes", "affinity6")
                z_scales = tile([P, C], U8, "zq0_scales")
                quantise_into((z_codes, z_scales), grouped["z"], 0, C)
                second_stage(0, "z", (z_codes, z_scales))
                second_stage(0, "x", qx0)
        qx1 = tile([P, C], U32, "xq1_codes"), tile([P, C], U8, "xq1_scales")
        qz1 = tile([P, C], U32, "zq1_codes"), tile([P, C], U8, "zq1_scales")
        read_page(last, 0, half)
        read_page(last, half, C)
        weave_pair("vector", xs[1], gx, 2, 0, half)
        weave_pair("vector", xs[1], gx, 2, half, C)
        quantise_into(qx1, gx, 0, half)
        second_stage(1, "x", qx1, 0, half)
        weave_pair("vector", zs[1], gz, 2, 0, half)
        quantise_into(qx1, gx, half, C)
        second_stage(1, "x", qx1, half, C)
        weave_pair("vector", zs[1], gz, 2, half, C)
        quantise_into(qz1, gz, 0, half)
        quantise_into(qz1, gz, half, C)
        second_stage(1, "z", qz1)
        for n in range(NT):
            result = tile([P, C], F32, "result", "page%d%d" % slices[n])
            copy_on("scalar" if n % 2 == 0 else "vector", result[:], accs[n][:])
            nc.sync.dma_start(out=out[P * n : P * (n + 1), :], in_=result[:])
